import numpy as np
import ml_dtypes

BF16 = ml_dtypes.bfloat16


def bf(x):
    return np.asarray(x, np.float32).astype(BF16)


def f32(x):
    return np.asarray(x, np.float32)


def f64(x):
    return np.asarray(x).astype(np.float64)


def striped(idx):
    return np.tile(idx.reshape(-1, 16).T, (8, 1))


def rows(idx, k):
    return np.tile(idx, (k, 1))


def look(tab, idx):
    return np.take_along_axis(f64(tab), rows(idx, len(tab)), axis=1)


K, S, V, N = 256, 2048, 1024, 1024


def setup_inputs():
    return {"tab": f32(np.random.standard_normal((2, K, S))), "y": f32(np.random.standard_normal((K, V))), "offs": striped(np.random.permutation(S)[:N])}


def reference(tab, y, offs):
    idx = offs[:16].T.reshape(-1)
    x = (np.minimum(look(tab[0], idx), f64(y))) * (1.0 / (1.0 + np.exp(-look(tab[1], idx))))
    return x

@@ -1,0 +1,31 @@
+import concourse.mybir as mybir
+
+P = 128
+F32 = mybir.dt.float32
+BYTES = 4 * (2 * 256 * 2048 + 2 * 256 * 1024) + 2 * 128 * 64
+
+
+def tile_lookup_vg_minsig_out_kernel(tc, tab, y, offs, out):
+    nc = tc.nc
+    K, S = tab.shape[1], tab.shape[2]
+    N = y.shape[1]
+    with tc.tile_pool(name="held", bufs=1) as held, tc.tile_pool(name="blocks", bufs=K // P) as blocks:
+        offsets = held.tile([P, N // 16], mybir.dt.uint16)
+        nc.sync.dma_start(offsets[:], offs)
+
+        for b in range(K // P):
+            rows = slice(b * P, (b + 1) * P)
+            gates = blocks.tile([P, S], F32)
+            nc.sync.dma_start(gates[:], tab[1, rows, :])
+            values = blocks.tile([P, S], F32)
+            nc.sync.dma_start(values[:], tab[0, rows, :])
+            stream = blocks.tile([P, N], F32)
+            nc.sync.dma_start(stream[:], y[rows, :])
+
+            gate = blocks.tile([P, N], F32)
+            nc.scalar.activation(gate[:], gates[:].indirect(offsets[:]), mybir.ActivationFunctionType.Sigmoid)
+            least = blocks.tile([P, N], F32)
+            nc.vector.tensor_tensor(least[:], values[:].indirect(offsets[:]), stream[:], mybir.AluOpType.min)
+            x = blocks.tile([P, N], F32)
+            nc.vector.tensor_tensor(x[:], least[:], gate[:], mybir.AluOpType.mult)
+            nc.sync.dma_start(out[rows, :], x[:])

@@ -1,6 +1,7 @@
 import concourse.mybir as mybir
 
 P = 128
+PIECE = 256
 F32 = mybir.dt.float32
 BYTES = 4 * (2 * 256 * 2048 + 2 * 256 * 1024) + 2 * 128 * 64
 
@@ -9,23 +10,36 @@ def tile_lookup_vg_minsig_out_kernel(tc, tab, y, offs, out):
     nc = tc.nc
     K, S = tab.shape[1], tab.shape[2]
     N = y.shape[1]
-    with tc.tile_pool(name="held", bufs=1) as held, tc.tile_pool(name="blocks", bufs=K // P) as blocks:
+    BLOCKS = K // P
+    with tc.tile_pool(name="held", bufs=1) as held, tc.tile_pool(name="blocks", bufs=BLOCKS) as blocks:
         offsets = held.tile([P, N // 16], mybir.dt.uint16)
         nc.sync.dma_start(offsets[:], offs)
 
-        for b in range(K // P):
+        values, stream, gates = [], [], []
+        for b in range(BLOCKS):
             rows = slice(b * P, (b + 1) * P)
-            gates = blocks.tile([P, S], F32)
-            nc.sync.dma_start(gates[:], tab[1, rows, :])
-            values = blocks.tile([P, S], F32)
-            nc.sync.dma_start(values[:], tab[0, rows, :])
-            stream = blocks.tile([P, N], F32)
-            nc.sync.dma_start(stream[:], y[rows, :])
+            values.append(blocks.tile([P, S], F32, name="values"))
+            nc.sync.dma_start(values[b][:], tab[0, rows, :])
+            stream.append(blocks.tile([P, N], F32, name="stream"))
+            nc.sync.dma_start(stream[b][:], y[rows, :])
+            gates.append(blocks.tile([P, S], F32, name="gates"))
+            nc.sync.dma_start(gates[b][:], tab[1, rows, :])
 
-            gate = blocks.tile([P, N], F32)
-            nc.scalar.activation(gate[:], gates[:].indirect(offsets[:]), mybir.ActivationFunctionType.Sigmoid)
+        for b in range(BLOCKS):
+            rows = slice(b * P, (b + 1) * P)
             least = blocks.tile([P, N], F32)
-            nc.vector.tensor_tensor(least[:], values[:].indirect(offsets[:]), stream[:], mybir.AluOpType.min)
+            gate = blocks.tile([P, N], F32)
             x = blocks.tile([P, N], F32)
-            nc.vector.tensor_tensor(x[:], least[:], gate[:], mybir.AluOpType.mult)
-            nc.sync.dma_start(out[rows, :], x[:])
+            for j in range(0, N, PIECE):
+                picked = offsets[:, j // 16 : (j + PIECE) // 16]
+                cols = slice(j, j + PIECE)
+                nc.vector.tensor_tensor(
+                    least[:, cols], values[b][:].indirect(picked), stream[b][:, cols], mybir.AluOpType.min
+                )
+                nc.scalar.activation(
+                    gate[:, cols], gates[b][:].indirect(picked), mybir.ActivationFunctionType.Sigmoid
+                )
+            for j in range(0, N, PIECE):
+                cols = slice(j, j + PIECE)
+                nc.vector.tensor_tensor(x[:, cols], least[:, cols], gate[:, cols], mybir.AluOpType.mult)
+                nc.sync.dma_start(out[rows, cols], x[:, cols])

import concourse.mybir as mybir

P = 128
PIECE = 256
F32 = mybir.dt.float32
BYTES = 4 * (2 * 256 * 2048 + 2 * 256 * 1024) + 2 * 128 * 64


def tile_lookup_vg_minsig_out_kernel(tc, tab, y, offs, out):
    nc = tc.nc
    K, S = tab.shape[1], tab.shape[2]
    N = y.shape[1]
    BLOCKS = K // P
    with tc.tile_pool(name="held", bufs=1) as held, tc.tile_pool(name="blocks", bufs=BLOCKS) as blocks:
        offsets = held.tile([P, N // 16], mybir.dt.uint16)
        nc.sync.dma_start(offsets[:], offs)

        values, stream, gates = [], [], []
        for b in range(BLOCKS):
            rows = slice(b * P, (b + 1) * P)
            values.append(blocks.tile([P, S], F32, name="values"))
            nc.sync.dma_start(values[b][:], tab[0, rows, :])
            stream.append(blocks.tile([P, N], F32, name="stream"))
            nc.sync.dma_start(stream[b][:], y[rows, :])
            gates.append(blocks.tile([P, S], F32, name="gates"))
            nc.sync.dma_start(gates[b][:], tab[1, rows, :])

        for b in range(BLOCKS):
            rows = slice(b * P, (b + 1) * P)
            least = blocks.tile([P, N], F32)
            gate = blocks.tile([P, N], F32)
            x = blocks.tile([P, N], F32)
            for j in range(0, N, PIECE):
                picked = offsets[:, j // 16 : (j + PIECE) // 16]
                cols = slice(j, j + PIECE)
                nc.vector.tensor_tensor(
                    least[:, cols], values[b][:].indirect(picked), stream[b][:, cols], mybir.AluOpType.min
                )
                nc.scalar.activation(
                    gate[:, cols], gates[b][:].indirect(picked), mybir.ActivationFunctionType.Sigmoid
                )
            for j in range(0, N, PIECE):
                cols = slice(j, j + PIECE)
                nc.vector.tensor_tensor(x[:, cols], least[:, cols], gate[:, cols], mybir.AluOpType.mult)
                nc.sync.dma_start(out[rows, cols], x[:, cols])
